import numpy as np
import ml_dtypes


def mxq(x, axis, fmt="e4m3"):
    dtype, down = {"e4m3": (ml_dtypes.float8_e4m3fn, 7), "e5m2": (ml_dtypes.float8_e5m2, 14)}[fmt]
    v = np.moveaxis(np.asarray(x, np.float32).astype(ml_dtypes.bfloat16).astype(np.float64), axis, -1)
    blocks = v.reshape(v.shape[:-1] + (-1, 32))
    amax = np.abs(blocks).max(-1, keepdims=True)
    byte = np.maximum(np.where(amax > 0, np.frexp(amax)[1] - 1 + 127, 0) - down, 1)
    scale = np.exp2(byte - 127.0)
    codes = (blocks / scale).astype(np.float32).astype(dtype).astype(np.float64)
    return np.moveaxis((codes * scale).reshape(v.shape), -1, axis)


WIDE = False


def mx_kscale(k):
    if not WIDE:
        return np.ones(k)
    levels = np.array([10, -10, 5, -5, 0])
    if k % 512:
        return np.exp2(np.random.permutation(np.resize(levels, k // 32))).repeat(32)
    a = np.empty((k // 512, 16))
    for p in range(k // 512):
        a[p, :8] = np.random.permutation(np.resize(levels, 8))
        for g in range(8):
            far = levels[np.abs(levels - a[p, g]) >= 10]
            a[p, g + 8] = far[np.random.randint(len(far))]
    return np.exp2(a.ravel()).repeat(32)


def f64(x):
    return np.asarray(x).astype(np.float64)


def striped(idx):
    return np.tile(np.asarray(idx).reshape(-1, 16).T, (8, 1)).astype(np.uint16)


def unstriped(offs):
    return offs[:16].T.reshape(-1).astype(np.int64)


E2M1 = np.array([0.0, 0.5, 1.0, 1.5, 2.0, 3.0, 4.0, 6.0, -0.0, -0.5, -1.0, -1.5, -2.0, -3.0, -4.0, -6.0])


def pack_weight(w, fmt):
    k, n = w.shape
    w = f64(np.asarray(w, np.float32).astype(ml_dtypes.bfloat16)).reshape(k // 32, 32, n)
    amax = np.abs(w).max(1)
    if fmt == "e4m3":
        byte = np.frexp(amax)[1] - 1 + 127 - 7
    else:
        mant, ex = np.frexp(amax / 6.0)
        byte = np.where(mant > 0.5, ex, ex - 1) + 127
    byte = np.clip(np.where(amax > 0, byte, 1), 1, 254)
    scaled = (w * np.exp2(127.0 - byte)[:, None, :]).reshape(k, n).astype(np.float32)
    by_word = np.ascontiguousarray(scaled.reshape(k // 512, 128, 4, n).transpose(0, 1, 3, 2))
    if fmt == "e4m3":
        words = by_word.astype(ml_dtypes.float8_e4m3fn).view(np.uint8)
    else:
        c = by_word.astype(ml_dtypes.float4_e2m1fn).view(np.uint8) & 0xF
        words = (c[..., 0::2] | (c[..., 1::2] << 4)).reshape(k // 512, 128, 2 * n)
    return np.ascontiguousarray(words), np.ascontiguousarray(byte.astype(np.uint8).reshape(k // 512, 16, n))


def unpack_weight(words, scales, fmt):
    g, _, n = scales.shape
    words = np.ascontiguousarray(words).reshape(g, 128, n, -1)
    if fmt == "e4m3":
        vals = words.view(ml_dtypes.float8_e4m3fn).astype(np.float64)
    else:
        nib = np.empty((g, 128, n, 4), np.uint8)
        nib[..., 0::2] = words & 0xF
        nib[..., 1::2] = words >> 4
        vals = E2M1[nib]
    vals = vals * np.repeat(np.exp2(scales.astype(np.float64) - 127.0), 8, axis=1)[..., None]
    return vals.transpose(0, 1, 3, 2).reshape(g * 512, n)


B, N, T, D, DV, NQ = 1, 512, 1024, 1024, 128, 256


def setup_inputs():
    n = np.random.standard_normal
    idx = np.sort(np.random.permutation(T)[:B * N].reshape(B, N), axis=1).reshape(-1)
    s = mx_kscale(D)[:, None]
    u = np.ones(T)
    u[idx] = mx_kscale(B * N)
    r = np.random.uniform(0.5, 2.0, T)
    qp = [pack_weight(x, "e4m3") for x in n((B, D, NQ)) * s * (0.80 / np.sqrt(D))]
    k = n((D, T)) / s
    v = n((DV, T)) / (u * r)
    kp = pack_weight(k, "e2m1")
    when = np.zeros(T)
    when[idx] = np.sort(np.random.permutation(2 * N)[:B * N])
    return {
        "q_words": np.stack([x[0] for x in qp]),
        "q_scales": np.stack([x[1] for x in qp]),
        "k_words": np.ascontiguousarray(kp[0].reshape(D // 1024, 2, 128, T, 2).transpose(0, 2, 3, 1, 4)).reshape(D // 1024, 128, T, 4),
        "k_scales": kp[1],
        "vT": v.astype(np.float32),
        "vs": np.tile(u * r, (128, 1)).astype(np.float32),
        "pos": np.tile(when, (128, 1)).astype(np.float32),
        "slope": np.exp2(-np.random.randint(8, 13, (B, NQ, 1))).astype(np.float32),
        "sink": (2.0 + 3.0 * n((B, NQ, 1))).astype(np.float32),
        "offs": striped(idx),
    }


def reference(q_words, q_scales, k_words, k_scales, vT, vs, pos, slope, sink, offs):
    idx = unstriped(offs)
    k = unpack_weight(k_words.reshape(D // 1024, 128, T, 2, 2).transpose(0, 3, 1, 2, 4).reshape(D // 512, 128, 2 * T), k_scales, "e2m1")
    v = f64(vT)
    pick = lambda x: x[:, idx].reshape(x.shape[0], B, N).transpose(1, 0, 2)
    q = np.stack([unpack_weight(q_words[b], q_scales[b], "e4m3") for b in range(B)])
    score = q.transpose(0, 2, 1) @ pick(k)
    score = score + f64(slope) * pick(f64(pos))[:, :1, :]
    m = np.maximum(score.max(-1, keepdims=True), f64(sink))
    p = np.exp(score - m)
    total = p.sum(-1, keepdims=True) + np.exp(f64(sink) - m)
    w = p * pick(f64(vs))[:, :1, :]
    y = mxq(w, 2, "e4m3") @ mxq(pick(v).transpose(0, 2, 1), 1, "e4m3")
    y = y / total
    return y

@@ -1,0 +1,173 @@
+from contextlib import ExitStack
+
+import concourse.mybir as mybir
+from concourse.masks import make_identity
+
+F32 = mybir.dt.float32
+BF16 = mybir.dt.bfloat16
+I32 = mybir.dt.int32
+U32 = mybir.dt.uint32
+U16 = mybir.dt.uint16
+U8 = mybir.dt.uint8
+FP8X4 = mybir.dt.float8_e4m3fn_x4
+FP4X4 = mybir.dt.float4_e2m1fn_x4
+ALU = mybir.AluOpType
+ACT = mybir.ActivationFunctionType
+
+P = 128
+N, T, D, DV, NQ = 512, 1024, 1024, 128, 256
+PASSES = D // 512
+QT = NQ // P
+SHIFT = 16
+
+FLOPS = 2 * NQ * N * D + 2 * NQ * N * DV
+
+
+def tile_attend_soft_alibi_sink_srtq256n512t1024_kernel(tc, q_words, q_scales, k_words, k_scales, vT, vs, pos, slope, sink, offs, out):
+    nc = tc.nc
+    with ExitStack() as ctx:
+        sb = ctx.enter_context(tc.tile_pool(name="sb", bufs=1))
+        ps = ctx.enter_context(tc.psum_pool(name="ps", bufs=1))
+
+        offsets = sb.tile([P, N // 16], U16, name="offsets")
+        nc.sync.dma_start(offsets[:], offs)
+
+        ks_pool = sb.tile([P, T], U8, name="ks_pool", align_bytes=64)
+        nc.vector.memset(ks_pool[:].bitcast(I32), 0)
+        ks_rows = k_scales.rearrange("o (Q r) t -> r Q o t", r=4)
+        for r in range(4):
+            nc.scalar.dma_start(ks_pool[r:P:SHIFT, :].bitcast(I32), ks_rows[r].bitcast(I32))
+
+        kw_pool = sb.tile([P, T], U32, name="kw_pool", align_bytes=64)
+        nc.sync.dma_start(kw_pool[:].bitcast(I32), k_words[0].rearrange("p t b -> p (t b)").bitcast(I32))
+        v_f32 = sb.tile([P, T], F32, name="v_f32")
+        nc.sync.dma_start(v_f32[:], vT)
+        qw = sb.tile([P, PASSES, NQ], U32, name="qw", align_bytes=64)
+        nc.sync.dma_start(qw[:].bitcast(I32), q_words[0].rearrange("o p q b -> p o (q b)").bitcast(I32))
+
+        qs = sb.tile([P, PASSES, NQ], U8, name="qs", align_bytes=64)
+        nc.vector.memset(qs[:].bitcast(I32), 0)
+        qs_rows = q_scales[0].rearrange("o (Q r) q -> r Q o q", r=4)
+        for r in range(4):
+            nc.sync.dma_start(qs[r:P:32, :, :].bitcast(I32), qs_rows[r].bitcast(I32))
+
+        warm_in = sb.tile([P, 1], F32, name="warm_in", tag="pos")
+        warm_out = sb.tile([P, 1], F32, name="warm_out")
+        nc.vector.memset(warm_in[:], 0.0)
+        nc.scalar.activation(warm_out[:], warm_in[:], ACT.Exp)
+
+        vs_pool = sb.tile([P, T], F32, name="vs_pool")
+        nc.vector.memset(vs_pool[:], 0.0)
+        nc.sync.dma_start(vs_pool[0:1, :], vs[0:1, :])
+        pos_pool = sb.tile([P, T], F32, name="pos_pool", tag="pos")
+        nc.sync.dma_start(pos_pool[:], pos)
+
+        slope_c = sb.tile([P, QT], F32, name="slope_c")
+        sink_c = sb.tile([P, QT], F32, name="sink_c")
+        with nc.allow_non_contiguous_dma(reason="one float32 a query row"):
+            nc.gpsimd.dma_start(slope_c[:], slope[0].rearrange("(t p) o -> p (t o)", p=P))
+            nc.gpsimd.dma_start(sink_c[:], sink[0].rearrange("(t p) o -> p (t o)", p=P))
+
+        ks_hi = sb.tile([P, N], U8, name="ks_hi", align_bytes=64)
+        nc.gpsimd.memset(ks_hi[:].bitcast(I32), 0)
+        ident_f = sb.tile([P, P], F32, name="ident_f")
+        make_identity(nc, ident_f[:])
+        ident_b = sb.tile([P, P], BF16, name="ident_b")
+        make_identity(nc, ident_b[:])
+
+        ks_g = sb.tile([P, N], U8, name="ks_g", align_bytes=64)
+        nc.vector.tensor_copy(ks_g[:], ks_pool[:].indirect(offsets[:]))
+        for lo, hi in ((0, 64), (64, 96), (96, 112)):
+            nc.sync.dma_start(ks_hi[lo:hi, :].bitcast(I32), ks_g[lo + SHIFT : hi + SHIFT, :].bitcast(I32))
+        kw_g = sb.tile([P, N], U32, name="kw_g", align_bytes=64)
+        nc.vector.tensor_copy(kw_g[:], kw_pool[:].indirect(offsets[:]))
+        k_op = sb.tile([P, PASSES * N * 2], U8, name="k_op", align_bytes=64)
+        nc.vector.tensor_copy(
+            k_op[:].bitcast(U16).rearrange("p (o n) -> p o n", o=PASSES),
+            kw_g[:].bitcast(U16).rearrange("p (n o) -> p o n", o=PASSES),
+        )
+        vs_g = sb.tile([P, N], F32, name="vs_g")
+        nc.vector.tensor_copy(vs_g[:], vs_pool[:].indirect(offsets[:]))
+        pos_g = sb.tile([P, N], F32, name="pos_g")
+        nc.vector.tensor_copy(pos_g[:], pos_pool[:].indirect(offsets[:]))
+
+        k_planes = (ks_g, ks_hi)
+        scores = [ps.tile([P, N], F32, name="scores%d" % t) for t in range(QT)]
+        for t in range(QT):
+            cols = slice(t * P, (t + 1) * P)
+            for o in range(PASSES):
+                nc.tensor.matmul_mx(
+                    out=scores[t][:],
+                    lhsT=qw[:, o, cols].bitcast(FP8X4),
+                    lhsT_scale=qs[:, o, cols],
+                    rhs=k_op[:, o * 2 * N : (o + 1) * 2 * N].bitcast(FP4X4),
+                    rhs_scale=k_planes[o][:],
+                    start=(o == 0),
+                    stop=(o == PASSES - 1),
+                )
+
+        v_bf = sb.tile([P, T], BF16, name="v_bf")
+        nc.scalar.copy(v_bf[:], v_f32[:])
+        v_g = sb.tile([P, N], BF16, name="v_g")
+        nc.scalar.activation(v_g[:].rearrange("p (r g j) -> p g r j", r=4, j=8), v_bf[:].indirect(offsets[:]), ACT.Copy)
+        vs_d = sb.tile([P, N], F32, name="vs_d")
+        nc.scalar.copy(vs_d[:].rearrange("p (r g j) -> p g r j", r=4, j=8), vs_g[:].rearrange("p (g r j) -> p g r j", r=4, j=8))
+        v_t = ps.tile([P, 4, DV], BF16, name="v_t")
+        for r in range(4):
+            nc.tensor.transpose(v_t[:, r, :], v_g[:, r * P : (r + 1) * P], ident_b[:])
+        vs_t = ps.tile([P, 4, P], F32, name="vs_t")
+        for r in range(4):
+            nc.tensor.transpose(vs_t[:, r, :], vs_d[:, r * P : (r + 1) * P], ident_f[:])
+        v_i = sb.tile([P, DV, 4], BF16, name="v_i", align_bytes=64)
+        nc.scalar.copy(v_i[:], v_t[:].rearrange("p r e -> p e r"))
+        vs_c = sb.tile([P, 4], F32, name="vs_c")
+        nc.scalar.copy(vs_c[:], vs_t[:, :, 0])
+
+        neg = [sb.tile([P, N + 8], F32, name="neg%d" % t) for t in range(QT)]
+        prob = [sb.tile([P, N + 8], F32, name="prob%d" % t) for t in range(QT)]
+        neg_max = [sb.tile([P, 1], F32, name="neg_max%d" % t) for t in range(QT)]
+        total = [sb.tile([P, 1], F32, name="total%d" % t) for t in range(QT)]
+        p_t = [ps.tile([P, 4, P], F32, name="p_t%d" % t) for t in range(QT)]
+        for t in range(QT):
+            nc.gpsimd.tensor_scalar(neg[t][:, N : N + 1], sink_c[:, t : t + 1], -1.0, 0.0, ALU.mult, ALU.add)
+        for t in range(QT):
+            s = sb.tile([P, N], F32, name="s%d" % t)
+            nc.vector.scalar_tensor_tensor(s[:], pos_g[:], slope_c[:, t : t + 1], scores[t][:], ALU.mult, ALU.add)
+            nc.vector.tensor_scalar(
+                neg[t][:, 0:N].rearrange("p (r g j) -> p g r j", r=4, j=8),
+                s[:].rearrange("p (g r j) -> p g r j", r=4, j=8),
+                -1.0,
+                neg[t][:, N : N + 1],
+                ALU.mult,
+                ALU.min,
+                accum_out=neg_max[t][:],
+            )
+            nc.scalar.activation(prob[t][:, 0 : N + 1], neg[t][:, 0 : N + 1], ACT.Exp, bias=neg_max[t][:], scale=-1.0, accum_out=total[t][:])
+            for r in range(4):
+                nc.tensor.transpose(p_t[t][:, r, :], prob[t][:, r * P : (r + 1) * P], ident_f[:])
+
+        v_q = sb.tile([P, DV], U32, name="v_q", align_bytes=64)
+        v_s = sb.tile([P, DV], U8, name="v_s", align_bytes=64)
+        nc.vector.quantize_mx(out=v_q[:].bitcast(FP8X4), scales=v_s[:], in_=v_i[:].rearrange("p e r -> p (e r)"))
+
+        for t in range(QT):
+            w_i = sb.tile([P, P, 4], BF16, name="w_i%d" % t, align_bytes=64)
+            nc.vector.tensor_tensor(w_i[:], p_t[t][:].rearrange("p r q -> p q r"), vs_c[:].unsqueeze(1).to_broadcast([P, P, 4]), ALU.mult)
+            inv = sb.tile([P, 1], F32, name="inv%d" % t)
+            nc.vector.reciprocal(inv[:], total[t][:])
+            w_q = sb.tile([P, P], U32, name="w_q%d" % t, align_bytes=64)
+            w_s = sb.tile([P, P], U8, name="w_s%d" % t, align_bytes=64)
+            nc.vector.quantize_mx(out=w_q[:].bitcast(FP8X4), scales=w_s[:], in_=w_i[:].rearrange("p q r -> p (q r)"))
+            acc = ps.tile([P, DV], F32, name="acc%d" % t)
+            nc.tensor.matmul_mx(
+                out=acc[:],
+                lhsT=w_q[:].bitcast(FP8X4),
+                lhsT_scale=w_s[:],
+                rhs=v_q[:].bitcast(FP8X4),
+                rhs_scale=v_s[:],
+                start=True,
+                stop=True,
+            )
+            y = sb.tile([P, DV], F32, name="y%d" % t)
+            nc.scalar.activation(y[:], acc[:], ACT.Copy, scale=inv[:])
+            nc.sync.dma_start(out[0, t * P : (t + 1) * P, :], y[:])

@@ -36,12 +36,10 @@ def tile_attend_soft_alibi_sink_srtq256n512t1024_kernel(tc, q_words, q_scales, k
         nc.vector.memset(ks_pool[:].bitcast(I32), 0)
         ks_rows = k_scales.rearrange("o (Q r) t -> r Q o t", r=4)
         for r in range(4):
-            nc.scalar.dma_start(ks_pool[r:P:SHIFT, :].bitcast(I32), ks_rows[r].bitcast(I32))
+            (nc.scalar if r < 2 else nc.sync).dma_start(ks_pool[r:P:SHIFT, :].bitcast(I32), ks_rows[r].bitcast(I32))
 
         kw_pool = sb.tile([P, T], U32, name="kw_pool", align_bytes=64)
         nc.sync.dma_start(kw_pool[:].bitcast(I32), k_words[0].rearrange("p t b -> p (t b)").bitcast(I32))
-        v_f32 = sb.tile([P, T], F32, name="v_f32")
-        nc.sync.dma_start(v_f32[:], vT)
         qw = sb.tile([P, PASSES, NQ], U32, name="qw", align_bytes=64)
         nc.sync.dma_start(qw[:].bitcast(I32), q_words[0].rearrange("o p q b -> p o (q b)").bitcast(I32))
 
@@ -51,7 +49,7 @@ def tile_attend_soft_alibi_sink_srtq256n512t1024_kernel(tc, q_words, q_scales, k
         for r in range(4):
             nc.sync.dma_start(qs[r:P:32, :, :].bitcast(I32), qs_rows[r].bitcast(I32))
 
-        warm_in = sb.tile([P, 1], F32, name="warm_in", tag="pos")
+        warm_in = sb.tile([P, 1], F32, name="warm_in")
         warm_out = sb.tile([P, 1], F32, name="warm_out")
         nc.vector.memset(warm_in[:], 0.0)
         nc.scalar.activation(warm_out[:], warm_in[:], ACT.Exp)
@@ -59,7 +57,9 @@ def tile_attend_soft_alibi_sink_srtq256n512t1024_kernel(tc, q_words, q_scales, k
         vs_pool = sb.tile([P, T], F32, name="vs_pool")
         nc.vector.memset(vs_pool[:], 0.0)
         nc.sync.dma_start(vs_pool[0:1, :], vs[0:1, :])
-        pos_pool = sb.tile([P, T], F32, name="pos_pool", tag="pos")
+        v_f32 = sb.tile([P, T], F32, name="v_f32")
+        nc.sync.dma_start(v_f32[:], vT)
+        pos_pool = sb.tile([P, T], F32, name="pos_pool")
         nc.sync.dma_start(pos_pool[:], pos)
 
         slope_c = sb.tile([P, QT], F32, name="slope_c")
@@ -92,7 +92,7 @@ def tile_attend_soft_alibi_sink_srtq256n512t1024_kernel(tc, q_words, q_scales, k
         nc.vector.tensor_copy(pos_g[:], pos_pool[:].indirect(offsets[:]))
 
         k_planes = (ks_g, ks_hi)
-        scores = [ps.tile([P, N], F32, name="scores%d" % t) for t in range(QT)]
+        scores = [ps.tile([P, N], F32, name="scores%d" % t, tag="bank%d" % t) for t in range(QT)]
         for t in range(QT):
             cols = slice(t * P, (t + 1) * P)
             for o in range(PASSES):
@@ -111,28 +111,28 @@ def tile_attend_soft_alibi_sink_srtq256n512t1024_kernel(tc, q_words, q_scales, k
         v_g = sb.tile([P, N], BF16, name="v_g")
         nc.scalar.activation(v_g[:].rearrange("p (r g j) -> p g r j", r=4, j=8), v_bf[:].indirect(offsets[:]), ACT.Copy)
         vs_d = sb.tile([P, N], F32, name="vs_d")
-        nc.scalar.copy(vs_d[:].rearrange("p (r g j) -> p g r j", r=4, j=8), vs_g[:].rearrange("p (g r j) -> p g r j", r=4, j=8))
-        v_t = ps.tile([P, 4, DV], BF16, name="v_t")
-        for r in range(4):
-            nc.tensor.transpose(v_t[:, r, :], v_g[:, r * P : (r + 1) * P], ident_b[:])
-        vs_t = ps.tile([P, 4, P], F32, name="vs_t")
-        for r in range(4):
-            nc.tensor.transpose(vs_t[:, r, :], vs_d[:, r * P : (r + 1) * P], ident_f[:])
-        v_i = sb.tile([P, DV, 4], BF16, name="v_i", align_bytes=64)
-        nc.scalar.copy(v_i[:], v_t[:].rearrange("p r e -> p e r"))
-        vs_c = sb.tile([P, 4], F32, name="vs_c")
-        nc.scalar.copy(vs_c[:], vs_t[:, :, 0])
+        nc.gpsimd.tensor_copy(vs_d[:].rearrange("p (r g j) -> p g r j", r=4, j=8), vs_g[:].rearrange("p (g r j) -> p g r j", r=4, j=8))
 
         neg = [sb.tile([P, N + 8], F32, name="neg%d" % t) for t in range(QT)]
         prob = [sb.tile([P, N + 8], F32, name="prob%d" % t) for t in range(QT)]
         neg_max = [sb.tile([P, 1], F32, name="neg_max%d" % t) for t in range(QT)]
-        total = [sb.tile([P, 1], F32, name="total%d" % t) for t in range(QT)]
+        total = [sb.tile([P, 2], F32, name="total%d" % t) for t in range(QT)]
         p_t = [ps.tile([P, 4, P], F32, name="p_t%d" % t) for t in range(QT)]
         for t in range(QT):
             nc.gpsimd.tensor_scalar(neg[t][:, N : N + 1], sink_c[:, t : t + 1], -1.0, 0.0, ALU.mult, ALU.add)
+        biased = [sb.tile([P, N], F32, name="biased%d" % t) for t in range(QT)]
         for t in range(QT):
-            s = sb.tile([P, N], F32, name="s%d" % t)
-            nc.vector.scalar_tensor_tensor(s[:], pos_g[:], slope_c[:, t : t + 1], scores[t][:], ALU.mult, ALU.add)
+            nc.vector.scalar_tensor_tensor(biased[t][:], pos_g[:], slope_c[:, t : t + 1], scores[t][:], ALU.mult, ALU.add)
+        v_t = ps.tile([P, 4, DV], BF16, name="v_t", tag="bank0")
+        for r in range(4):
+            nc.tensor.transpose(v_t[:, r, :], v_g[:, r * P : (r + 1) * P], ident_b[:])
+        v_i = sb.tile([P, DV, 4], BF16, name="v_i", align_bytes=64)
+        nc.scalar.copy(v_i[:], v_t[:].rearrange("p r e -> p e r"))
+        vs_t = ps.tile([P, 4, P], F32, name="vs_t", tag="bank1")
+        for r in range(4):
+            nc.tensor.transpose(vs_t[:, r, :], vs_d[:, r * P : (r + 1) * P], ident_f[:])
+        for t in range(QT):
+            s = biased[t]
             nc.vector.tensor_scalar(
                 neg[t][:, 0:N].rearrange("p (r g j) -> p g r j", r=4, j=8),
                 s[:].rearrange("p (g r j) -> p g r j", r=4, j=8),
@@ -142,19 +142,26 @@ def tile_attend_soft_alibi_sink_srtq256n512t1024_kernel(tc, q_words, q_scales, k
                 ALU.min,
                 accum_out=neg_max[t][:],
             )
-            nc.scalar.activation(prob[t][:, 0 : N + 1], neg[t][:, 0 : N + 1], ACT.Exp, bias=neg_max[t][:], scale=-1.0, accum_out=total[t][:])
-            for r in range(4):
-                nc.tensor.transpose(p_t[t][:, r, :], prob[t][:, r * P : (r + 1) * P], ident_f[:])
+            for h, cols in enumerate((slice(0, N // 2), slice(N // 2, N + 1))):
+                nc.scalar.activation(prob[t][:, cols], neg[t][:, cols], ACT.Exp, bias=neg_max[t][:], scale=-1.0, accum_out=total[t][:, h : h + 1])
+                for r in (2 * h, 2 * h + 1):
+                    nc.tensor.transpose(p_t[t][:, r, :], prob[t][:, r * P : (r + 1) * P], ident_f[:])
 
+        vs_c = sb.tile([P, 4], F32, name="vs_c")
+        nc.vector.tensor_copy(vs_c[:], vs_t[:, :, 0])
         v_q = sb.tile([P, DV], U32, name="v_q", align_bytes=64)
         v_s = sb.tile([P, DV], U8, name="v_s", align_bytes=64)
         nc.vector.quantize_mx(out=v_q[:].bitcast(FP8X4), scales=v_s[:], in_=v_i[:].rearrange("p e r -> p (e r)"))
 
+        w_is = [sb.tile([P, P, 4], BF16, name="w_i%d" % t, align_bytes=64) for t in range(QT)]
         for t in range(QT):
-            w_i = sb.tile([P, P, 4], BF16, name="w_i%d" % t, align_bytes=64)
-            nc.vector.tensor_tensor(w_i[:], p_t[t][:].rearrange("p r q -> p q r"), vs_c[:].unsqueeze(1).to_broadcast([P, P, 4]), ALU.mult)
+            nc.vector.tensor_tensor(w_is[t][:], p_t[t][:].rearrange("p r q -> p q r"), vs_c[:].unsqueeze(1).to_broadcast([P, P, 4]), ALU.mult)
+        for t in range(QT):
+            w_i = w_is[t]
+            row_sum = sb.tile([P, 1], F32, name="row_sum%d" % t)
+            nc.gpsimd.tensor_tensor(row_sum[:], total[t][:, 0:1], total[t][:, 1:2], ALU.add)
             inv = sb.tile([P, 1], F32, name="inv%d" % t)
-            nc.vector.reciprocal(inv[:], total[t][:])
+            nc.vector.reciprocal(inv[:], row_sum[:])
             w_q = sb.tile([P, P], U32, name="w_q%d" % t, align_bytes=64)
             w_s = sb.tile([P, P], U8, name="w_s%d" % t, align_bytes=64)
             nc.vector.quantize_mx(out=w_q[:].bitcast(FP8X4), scales=w_s[:], in_=w_i[:].rearrange("p q r -> p (q r)"))

@@ -46,39 +46,41 @@ def tile_attend_soft_alibi_sink_srtq256n512t1024_kernel(tc, q_words, q_scales, k
         qs = sb.tile([P, PASSES, NQ], U8, name="qs", align_bytes=64)
         nc.vector.memset(qs[:].bitcast(I32), 0)
         qs_rows = q_scales[0].rearrange("o (Q r) q -> r Q o q", r=4)
-        for r in range(4):
-            nc.sync.dma_start(qs[r:P:32, :, :].bitcast(I32), qs_rows[r].bitcast(I32))
+        for r in range(2):
+            nc.scalar.dma_start(qs[r:P:32, :, :].bitcast(I32), qs_rows[r].bitcast(I32))
 
         warm_in = sb.tile([P, 1], F32, name="warm_in")
         warm_out = sb.tile([P, 1], F32, name="warm_out")
         nc.vector.memset(warm_in[:], 0.0)
         nc.scalar.activation(warm_out[:], warm_in[:], ACT.Exp)
+        for r in range(2, 4):
+            nc.scalar.dma_start(qs[r:P:32, :, :].bitcast(I32), qs_rows[r].bitcast(I32))
 
         vs_pool = sb.tile([P, T], F32, name="vs_pool")
         nc.vector.memset(vs_pool[:], 0.0)
-        nc.sync.dma_start(vs_pool[0:1, :], vs[0:1, :])
         v_f32 = sb.tile([P, T], F32, name="v_f32")
         nc.sync.dma_start(v_f32[:], vT)
+        nc.sync.dma_start(vs_pool[0:1, :], vs[0:1, :])
         pos_pool = sb.tile([P, T], F32, name="pos_pool")
         nc.sync.dma_start(pos_pool[:], pos)
 
-        slope_c = sb.tile([P, QT], F32, name="slope_c")
-        sink_c = sb.tile([P, QT], F32, name="sink_c")
-        with nc.allow_non_contiguous_dma(reason="one float32 a query row"):
-            nc.gpsimd.dma_start(slope_c[:], slope[0].rearrange("(t p) o -> p (t o)", p=P))
-            nc.gpsimd.dma_start(sink_c[:], sink[0].rearrange("(t p) o -> p (t o)", p=P))
-
-        ks_hi = sb.tile([P, N], U8, name="ks_hi", align_bytes=64)
-        nc.gpsimd.memset(ks_hi[:].bitcast(I32), 0)
         ident_f = sb.tile([P, P], F32, name="ident_f")
         make_identity(nc, ident_f[:])
         ident_b = sb.tile([P, P], BF16, name="ident_b")
         make_identity(nc, ident_b[:])
+        slope_c = sb.tile([P, QT], F32, name="slope_c")
+        sink_c = sb.tile([P, QT], F32, name="sink_c")
+        with nc.allow_non_contiguous_dma(reason="one float32 a query row"):
+            nc.sync.dma_start(slope_c[:], slope[0].rearrange("(t p) o -> p (t o)", p=P))
+            nc.sync.dma_start(sink_c[:], sink[0].rearrange("(t p) o -> p (t o)", p=P))
+
+        ks_hi = sb.tile([P, N], U8, name="ks_hi", align_bytes=64)
+        nc.vector.memset(ks_hi[:].bitcast(I32), 0)
 
         ks_g = sb.tile([P, N], U8, name="ks_g", align_bytes=64)
         nc.vector.tensor_copy(ks_g[:], ks_pool[:].indirect(offsets[:]))
         for lo, hi in ((0, 64), (64, 96), (96, 112)):
-            nc.sync.dma_start(ks_hi[lo:hi, :].bitcast(I32), ks_g[lo + SHIFT : hi + SHIFT, :].bitcast(I32))
+            nc.scalar.dma_start(ks_hi[lo:hi, :].bitcast(I32), ks_g[lo + SHIFT : hi + SHIFT, :].bitcast(I32))
         kw_g = sb.tile([P, N], U32, name="kw_g", align_bytes=64)
         nc.vector.tensor_copy(kw_g[:], kw_pool[:].indirect(offsets[:]))
         k_op = sb.tile([P, PASSES * N * 2], U8, name="k_op", align_bytes=64)
@@ -111,7 +113,7 @@ def tile_attend_soft_alibi_sink_srtq256n512t1024_kernel(tc, q_words, q_scales, k
         v_g = sb.tile([P, N], BF16, name="v_g")
         nc.scalar.activation(v_g[:].rearrange("p (r g j) -> p g r j", r=4, j=8), v_bf[:].indirect(offsets[:]), ACT.Copy)
         vs_d = sb.tile([P, N], F32, name="vs_d")
-        nc.gpsimd.tensor_copy(vs_d[:].rearrange("p (r g j) -> p g r j", r=4, j=8), vs_g[:].rearrange("p (g r j) -> p g r j", r=4, j=8))
+        nc.scalar.copy(vs_d[:].rearrange("p (r g j) -> p g r j", r=4, j=8), vs_g[:].rearrange("p (g r j) -> p g r j", r=4, j=8))
 
         neg = [sb.tile([P, N + 8], F32, name="neg%d" % t) for t in range(QT)]
         prob = [sb.tile([P, N + 8], F32, name="prob%d" % t) for t in range(QT)]
@@ -119,7 +121,7 @@ def tile_attend_soft_alibi_sink_srtq256n512t1024_kernel(tc, q_words, q_scales, k
         total = [sb.tile([P, 2], F32, name="total%d" % t) for t in range(QT)]
         p_t = [ps.tile([P, 4, P], F32, name="p_t%d" % t) for t in range(QT)]
         for t in range(QT):
-            nc.gpsimd.tensor_scalar(neg[t][:, N : N + 1], sink_c[:, t : t + 1], -1.0, 0.0, ALU.mult, ALU.add)
+            nc.scalar.activation(neg[t][:, N : N + 1], sink_c[:, t : t + 1], ACT.Copy, scale=-1.0)
         biased = [sb.tile([P, N], F32, name="biased%d" % t) for t in range(QT)]
         for t in range(QT):
             nc.vector.scalar_tensor_tensor(biased[t][:], pos_g[:], slope_c[:, t : t + 1], scores[t][:], ALU.mult, ALU.add)
@@ -159,7 +161,7 @@ def tile_attend_soft_alibi_sink_srtq256n512t1024_kernel(tc, q_words, q_scales, k
         for t in range(QT):
             w_i = w_is[t]
             row_sum = sb.tile([P, 1], F32, name="row_sum%d" % t)
-            nc.gpsimd.tensor_tensor(row_sum[:], total[t][:, 0:1], total[t][:, 1:2], ALU.add)
+            nc.scalar.activation(row_sum[:], total[t][:, 0:1], ACT.Identity, bias=total[t][:, 1:2])
             inv = sb.tile([P, 1], F32, name="inv%d" % t)
             nc.vector.reciprocal(inv[:], row_sum[:])
             w_q = sb.tile([P, P], U32, name="w_q%d" % t, align_bytes=64)
@@ -177,4 +179,4 @@ def tile_attend_soft_alibi_sink_srtq256n512t1024_kernel(tc, q_words, q_scales, k
             )
             y = sb.tile([P, DV], F32, name="y%d" % t)
             nc.scalar.activation(y[:], acc[:], ACT.Copy, scale=inv[:])
-            nc.sync.dma_start(out[0, t * P : (t + 1) * P, :], y[:])
+            (nc.sync if t == 0 else nc.scalar).dma_start(out[0, t * P : (t + 1) * P, :], y[:])

from contextlib import ExitStack

import concourse.mybir as mybir
from concourse.masks import make_identity

F32 = mybir.dt.float32
BF16 = mybir.dt.bfloat16
I32 = mybir.dt.int32
U32 = mybir.dt.uint32
U16 = mybir.dt.uint16
U8 = mybir.dt.uint8
FP8X4 = mybir.dt.float8_e4m3fn_x4
FP4X4 = mybir.dt.float4_e2m1fn_x4
ALU = mybir.AluOpType
ACT = mybir.ActivationFunctionType

P = 128
N, T, D, DV, NQ = 512, 1024, 1024, 128, 256
PASSES = D // 512
QT = NQ // P
SHIFT = 16

FLOPS = 2 * NQ * N * D + 2 * NQ * N * DV


def tile_attend_soft_alibi_sink_srtq256n512t1024_kernel(tc, q_words, q_scales, k_words, k_scales, vT, vs, pos, slope, sink, offs, out):
    nc = tc.nc
    with ExitStack() as ctx:
        sb = ctx.enter_context(tc.tile_pool(name="sb", bufs=1))
        ps = ctx.enter_context(tc.psum_pool(name="ps", bufs=1))

        offsets = sb.tile([P, N // 16], U16, name="offsets")
        nc.sync.dma_start(offsets[:], offs)

        ks_pool = sb.tile([P, T], U8, name="ks_pool", align_bytes=64)
        nc.vector.memset(ks_pool[:].bitcast(I32), 0)
        ks_rows = k_scales.rearrange("o (Q r) t -> r Q o t", r=4)
        for r in range(4):
            (nc.scalar if r < 2 else nc.sync).dma_start(ks_pool[r:P:SHIFT, :].bitcast(I32), ks_rows[r].bitcast(I32))

        kw_pool = sb.tile([P, T], U32, name="kw_pool", align_bytes=64)
        nc.sync.dma_start(kw_pool[:].bitcast(I32), k_words[0].rearrange("p t b -> p (t b)").bitcast(I32))
        qw = sb.tile([P, PASSES, NQ], U32, name="qw", align_bytes=64)
        nc.sync.dma_start(qw[:].bitcast(I32), q_words[0].rearrange("o p q b -> p o (q b)").bitcast(I32))

        qs = sb.tile([P, PASSES, NQ], U8, name="qs", align_bytes=64)
        nc.vector.memset(qs[:].bitcast(I32), 0)
        qs_rows = q_scales[0].rearrange("o (Q r) q -> r Q o q", r=4)
        for r in range(2):
            nc.scalar.dma_start(qs[r:P:32, :, :].bitcast(I32), qs_rows[r].bitcast(I32))

        warm_in = sb.tile([P, 1], F32, name="warm_in")
        warm_out = sb.tile([P, 1], F32, name="warm_out")
        nc.vector.memset(warm_in[:], 0.0)
        nc.scalar.activation(warm_out[:], warm_in[:], ACT.Exp)
        for r in range(2, 4):
            nc.scalar.dma_start(qs[r:P:32, :, :].bitcast(I32), qs_rows[r].bitcast(I32))

        vs_pool = sb.tile([P, T], F32, name="vs_pool")
        nc.vector.memset(vs_pool[:], 0.0)
        v_f32 = sb.tile([P, T], F32, name="v_f32")
        nc.sync.dma_start(v_f32[:], vT)
        nc.sync.dma_start(vs_pool[0:1, :], vs[0:1, :])
        pos_pool = sb.tile([P, T], F32, name="pos_pool")
        nc.sync.dma_start(pos_pool[:], pos)

        ident_f = sb.tile([P, P], F32, name="ident_f")
        make_identity(nc, ident_f[:])
        ident_b = sb.tile([P, P], BF16, name="ident_b")
        make_identity(nc, ident_b[:])
        slope_c = sb.tile([P, QT], F32, name="slope_c")
        sink_c = sb.tile([P, QT], F32, name="sink_c")
        with nc.allow_non_contiguous_dma(reason="one float32 a query row"):
            nc.sync.dma_start(slope_c[:], slope[0].rearrange("(t p) o -> p (t o)", p=P))
            nc.sync.dma_start(sink_c[:], sink[0].rearrange("(t p) o -> p (t o)", p=P))

        ks_hi = sb.tile([P, N], U8, name="ks_hi", align_bytes=64)
        nc.vector.memset(ks_hi[:].bitcast(I32), 0)

        ks_g = sb.tile([P, N], U8, name="ks_g", align_bytes=64)
        nc.vector.tensor_copy(ks_g[:], ks_pool[:].indirect(offsets[:]))
        for lo, hi in ((0, 64), (64, 96), (96, 112)):
            nc.scalar.dma_start(ks_hi[lo:hi, :].bitcast(I32), ks_g[lo + SHIFT : hi + SHIFT, :].bitcast(I32))
        kw_g = sb.tile([P, N], U32, name="kw_g", align_bytes=64)
        nc.vector.tensor_copy(kw_g[:], kw_pool[:].indirect(offsets[:]))
        k_op = sb.tile([P, PASSES * N * 2], U8, name="k_op", align_bytes=64)
        nc.vector.tensor_copy(
            k_op[:].bitcast(U16).rearrange("p (o n) -> p o n", o=PASSES),
            kw_g[:].bitcast(U16).rearrange("p (n o) -> p o n", o=PASSES),
        )
        vs_g = sb.tile([P, N], F32, name="vs_g")
        nc.vector.tensor_copy(vs_g[:], vs_pool[:].indirect(offsets[:]))
        pos_g = sb.tile([P, N], F32, name="pos_g")
        nc.vector.tensor_copy(pos_g[:], pos_pool[:].indirect(offsets[:]))

        k_planes = (ks_g, ks_hi)
        scores = [ps.tile([P, N], F32, name="scores%d" % t, tag="bank%d" % t) for t in range(QT)]
        for t in range(QT):
            cols = slice(t * P, (t + 1) * P)
            for o in range(PASSES):
                nc.tensor.matmul_mx(
                    out=scores[t][:],
                    lhsT=qw[:, o, cols].bitcast(FP8X4),
                    lhsT_scale=qs[:, o, cols],
                    rhs=k_op[:, o * 2 * N : (o + 1) * 2 * N].bitcast(FP4X4),
                    rhs_scale=k_planes[o][:],
                    start=(o == 0),
                    stop=(o == PASSES - 1),
                )

        v_bf = sb.tile([P, T], BF16, name="v_bf")
        nc.scalar.copy(v_bf[:], v_f32[:])
        v_g = sb.tile([P, N], BF16, name="v_g")
        nc.scalar.activation(v_g[:].rearrange("p (r g j) -> p g r j", r=4, j=8), v_bf[:].indirect(offsets[:]), ACT.Copy)
        vs_d = sb.tile([P, N], F32, name="vs_d")
        nc.scalar.copy(vs_d[:].rearrange("p (r g j) -> p g r j", r=4, j=8), vs_g[:].rearrange("p (g r j) -> p g r j", r=4, j=8))

        neg = [sb.tile([P, N + 8], F32, name="neg%d" % t) for t in range(QT)]
        prob = [sb.tile([P, N + 8], F32, name="prob%d" % t) for t in range(QT)]
        neg_max = [sb.tile([P, 1], F32, name="neg_max%d" % t) for t in range(QT)]
        total = [sb.tile([P, 2], F32, name="total%d" % t) for t in range(QT)]
        p_t = [ps.tile([P, 4, P], F32, name="p_t%d" % t) for t in range(QT)]
        for t in range(QT):
            nc.scalar.activation(neg[t][:, N : N + 1], sink_c[:, t : t + 1], ACT.Copy, scale=-1.0)
        biased = [sb.tile([P, N], F32, name="biased%d" % t) for t in range(QT)]
        for t in range(QT):
            nc.vector.scalar_tensor_tensor(biased[t][:], pos_g[:], slope_c[:, t : t + 1], scores[t][:], ALU.mult, ALU.add)
        v_t = ps.tile([P, 4, DV], BF16, name="v_t", tag="bank0")
        for r in range(4):
            nc.tensor.transpose(v_t[:, r, :], v_g[:, r * P : (r + 1) * P], ident_b[:])
        v_i = sb.tile([P, DV, 4], BF16, name="v_i", align_bytes=64)
        nc.scalar.copy(v_i[:], v_t[:].rearrange("p r e -> p e r"))
        vs_t = ps.tile([P, 4, P], F32, name="vs_t", tag="bank1")
        for r in range(4):
            nc.tensor.transpose(vs_t[:, r, :], vs_d[:, r * P : (r + 1) * P], ident_f[:])
        for t in range(QT):
            s = biased[t]
            nc.vector.tensor_scalar(
                neg[t][:, 0:N].rearrange("p (r g j) -> p g r j", r=4, j=8),
                s[:].rearrange("p (g r j) -> p g r j", r=4, j=8),
                -1.0,
                neg[t][:, N : N + 1],
                ALU.mult,
                ALU.min,
                accum_out=neg_max[t][:],
            )
            for h, cols in enumerate((slice(0, N // 2), slice(N // 2, N + 1))):
                nc.scalar.activation(prob[t][:, cols], neg[t][:, cols], ACT.Exp, bias=neg_max[t][:], scale=-1.0, accum_out=total[t][:, h : h + 1])
                for r in (2 * h, 2 * h + 1):
                    nc.tensor.transpose(p_t[t][:, r, :], prob[t][:, r * P : (r + 1) * P], ident_f[:])

        vs_c = sb.tile([P, 4], F32, name="vs_c")
        nc.vector.tensor_copy(vs_c[:], vs_t[:, :, 0])
        v_q = sb.tile([P, DV], U32, name="v_q", align_bytes=64)
        v_s = sb.tile([P, DV], U8, name="v_s", align_bytes=64)
        nc.vector.quantize_mx(out=v_q[:].bitcast(FP8X4), scales=v_s[:], in_=v_i[:].rearrange("p e r -> p (e r)"))

        w_is = [sb.tile([P, P, 4], BF16, name="w_i%d" % t, align_bytes=64) for t in range(QT)]
        for t in range(QT):
            nc.vector.tensor_tensor(w_is[t][:], p_t[t][:].rearrange("p r q -> p q r"), vs_c[:].unsqueeze(1).to_broadcast([P, P, 4]), ALU.mult)
        for t in range(QT):
            w_i = w_is[t]
            row_sum = sb.tile([P, 1], F32, name="row_sum%d" % t)
            nc.scalar.activation(row_sum[:], total[t][:, 0:1], ACT.Identity, bias=total[t][:, 1:2])
            inv = sb.tile([P, 1], F32, name="inv%d" % t)
            nc.vector.reciprocal(inv[:], row_sum[:])
            w_q = sb.tile([P, P], U32, name="w_q%d" % t, align_bytes=64)
            w_s = sb.tile([P, P], U8, name="w_s%d" % t, align_bytes=64)
            nc.vector.quantize_mx(out=w_q[:].bitcast(FP8X4), scales=w_s[:], in_=w_i[:].rearrange("p q r -> p (q r)"))
            acc = ps.tile([P, DV], F32, name="acc%d" % t)
            nc.tensor.matmul_mx(
                out=acc[:],
                lhsT=w_q[:].bitcast(FP8X4),
                lhsT_scale=w_s[:],
                rhs=v_q[:].bitcast(FP8X4),
                rhs_scale=v_s[:],
                start=True,
                stop=True,
            )
            y = sb.tile([P, DV], F32, name="y%d" % t)
            nc.scalar.activation(y[:], acc[:], ACT.Copy, scale=inv[:])
            (nc.sync if t == 0 else nc.scalar).dma_start(out[0, t * P : (t + 1) * P, :], y[:])
